import numpy as np
import ml_dtypes


def mxq(x, axis, fmt="e4m3"):
    dtype, down = {"e4m3": (ml_dtypes.float8_e4m3fn, 7), "e5m2": (ml_dtypes.float8_e5m2, 14)}[fmt]
    v = np.moveaxis(np.asarray(x, np.float32).astype(ml_dtypes.bfloat16).astype(np.float64), axis, -1)
    blocks = v.reshape(v.shape[:-1] + (-1, 32))
    amax = np.abs(blocks).max(-1, keepdims=True)
    byte = np.maximum(np.where(amax > 0, np.frexp(amax)[1] - 1 + 127, 0) - down, 1)
    scale = np.exp2(byte - 127.0)
    codes = (blocks / scale).astype(np.float32).astype(dtype).astype(np.float64)
    return np.moveaxis((codes * scale).reshape(v.shape), -1, axis)


WIDE = False


def mx_kscale(k):
    if not WIDE:
        return np.ones(k)
    levels = np.array([10, -10, 5, -5, 0])
    if k % 512:
        return np.exp2(np.random.permutation(np.resize(levels, k // 32))).repeat(32)
    a = np.empty((k // 512, 16))
    for p in range(k // 512):
        a[p, :8] = np.random.permutation(np.resize(levels, 8))
        for g in range(8):
            far = levels[np.abs(levels - a[p, g]) >= 10]
            a[p, g + 8] = far[np.random.randint(len(far))]
    return np.exp2(a.ravel()).repeat(32)


BF16 = ml_dtypes.bfloat16


def bf(x):
    return np.asarray(x, np.float32).astype(BF16)


def f64(x):
    return np.asarray(x).astype(np.float64)

E4M3FN = np.array([(-1.0 if i & 128 else 1.0) * ((1.0 + (i & 7) / 8.0) * 2.0 ** (((i >> 3) & 15) - 7) if i & 120 else (i & 7) * 2.0 ** -9) for i in range(256)])


def e4m3fn_bytes(y):
    return np.clip(np.asarray(y, np.float64), -448.0, 448.0).astype(np.float32).astype(ml_dtypes.float8_e4m3fn).view(np.uint8)


def e4m3fn_values(b):
    return E4M3FN[b]


O, NA, NB = 1024, 1024, 1536


def setup_inputs():
    s = mx_kscale(O)
    ca = np.random.standard_normal((O, NA)) / O ** 0.25 * s[:, None]
    ca_scale = (np.max(np.abs(ca), axis=1, keepdims=True) / 448.0).astype(np.float32)
    cb = np.random.standard_normal((O, NB)) / O ** 0.25 / s[:, None]
    eps = -(0.2 + 1.3 * np.random.random(O))
    return {"ca_bytes": e4m3fn_bytes(ca / f64(ca_scale)),
            "ca_scale": ca_scale,
            "cb": bf(cb),
            "eps": bf(eps)}


def reference(ca_bytes, ca_scale, cb, eps):
    ca = e4m3fn_values(ca_bytes) * np.repeat(f64(ca_scale), NA, axis=1)
    cb_e = f64(cb) * f64(eps)[:, None]
    qa = mxq(ca, 0, "e4m3")
    qb = mxq(f64(cb), 0, "e4m3")
    qe = mxq(cb_e, 0, "e4m3")
    p = 2.0 * (qa.T @ qb)
    w = 2.0 * (qa.T @ qe)
    return p, w

@@ -1,0 +1,166 @@
+from contextlib import ExitStack
+
+import concourse.mybir as mybir
+from concourse.masks import make_identity
+
+F32 = mybir.dt.float32
+BF16 = mybir.dt.bfloat16
+U32 = mybir.dt.uint32
+U8 = mybir.dt.uint8
+FP8 = mybir.dt.float8_e4m3fn
+FP8X4 = mybir.dt.float8_e4m3fn_x4
+COPY = mybir.ActivationFunctionType.Copy
+MULT = mybir.AluOpType.mult
+
+O, NA, NB = 1024, 1024, 1536
+FLOPS = 2 * 2 * O * NA * NB
+
+P = 128
+T = 4
+G = O // (P * T)
+NC = 512
+MT = NA // P
+
+
+def tile_density_and_energy_weighted_block_d3_kernel(tc, ca_bytes, ca_scale, cb, eps, out_p, out_w):
+    nc = tc.nc
+    with ExitStack() as ctx:
+        keep = ctx.enter_context(tc.tile_pool(name="keep", bufs=1))
+        stage = ctx.enter_context(tc.tile_pool(name="stage", bufs=1))
+        outs = ctx.enter_context(tc.tile_pool(name="outs", bufs=8))
+        psum = ctx.enter_context(tc.psum_pool(name="psum", bufs=8))
+        ctx.enter_context(tc.manual_schedule())
+
+        sc = keep.tile([P, G, T], F32, name="sc")
+        ep = keep.tile([P, G, T], BF16, name="ep")
+        nc.scalar.dma_start(out=sc[:], in_=ca_scale.rearrange("(g p t) o -> p g (t o)", p=P, t=T))
+        nc.scalar.dma_start(out=ep[:], in_=eps.rearrange("(g p t) -> p g t", p=P, t=T))
+        cav = ca_bytes.rearrange("(g p t) n -> g p t n", p=P, t=T)
+        cbv = cb.rearrange("(g p t) n -> g p t n", p=P, t=T)
+        byt = [keep.tile([P, T, NA], U8, name="byt%d" % g) for g in range(G)]
+        raw0 = [keep.tile([P, T, NC], BF16, name="rawa%d" % g) for g in range(G)]
+        raw1 = [keep.tile([P, T, 2 * NC], BF16, name="rawb%d" % g) for g in range(G)]
+        for g in range(G):
+            nc.sync.dma_start(out=byt[g][:], in_=cav[g])
+        for g in range(G):
+            nc.sync.dma_start(out=raw0[g][:], in_=cbv[g, :, :, 0:NC])
+        for g in range(G):
+            nc.sync.dma_start(out=raw1[g][:], in_=cbv[g, :, :, NC:3 * NC])
+
+        ident = keep.tile([P, P], BF16, name="ident")
+        make_identity(nc, ident[:])
+
+        ca_codes = keep.tile([P, G, NA], U32, name="ca_codes", align_bytes=64)
+        ca_scales = keep.tile([P, G, NA], U8, name="ca_scales", align_bytes=64)
+        cb_codes = keep.tile([P, 6, G, NC], U32, name="cb_codes", align_bytes=64)
+        cb_scales = keep.tile([P, 6, G, NC], U8, name="cb_scales", align_bytes=64)
+        wide = [keep.tile([P, T, NA], BF16, name="wide%d" % g) for g in range(G)]
+        nat = [keep.tile([P, NA, T], BF16, name="nat%d" % g, align_bytes=64) for g in range(G)]
+        cbn = [[keep.tile([P, NC, T], BF16, name="cbn%d_%d" % (c, g), align_bytes=64) for g in range(G)] for c in range(3)]
+        cen = [[stage.tile([P, NC, T], BF16, name="cen%d" % g, align_bytes=64, bufs=2) for g in range(G)] for c in range(3)]
+
+        H = NA // 2
+        banks = {}
+
+        def widen(g, h):
+            cols = slice(h * H, (h + 1) * H)
+            for t in (3, 0, 1, 2):
+                src = byt[g][:, t, cols].bitcast(FP8)
+                if t == 3:
+                    nc.scalar.activation(out=wide[g][:, t, cols], in_=src, func=COPY, scale=sc[:, g, t:t + 1])
+                else:
+                    nc.vector.tensor_scalar(out=wide[g][:, t, cols], in0=src, scalar1=sc[:, g, t:t + 1], scalar2=None, op0=MULT)
+
+        def turn(key, src, w0):
+            bank = psum.tile([P, 2, P, T], BF16, name="bank")
+            for i in range(2):
+                nc.tensor.matmul(
+                    out=bank[:, i], lhsT=ident[:],
+                    rhs=src[:, :, w0 + i * P:w0 + (i + 1) * P].rearrange("p t w -> p w t"),
+                    start=True, stop=True)
+            banks[key] = bank
+
+        def empty(key, dst, copy):
+            copy(out=dst, in_=banks[key][:].rearrange("p i w t -> p (i w) t"))
+
+        def turn_ca(g, h):
+            for w in range(2):
+                turn((g, h, w), wide[g], h * H + w * 256)
+
+        def empty_ca(g, h, w, copy):
+            w0 = h * H + w * 256
+            empty((g, h, w), nat[g][:, w0:w0 + 256, :], copy)
+
+        def turn_cb(g):
+            for w in range(2):
+                turn((g, w), raw0[g], w * 256)
+
+        def empty_cb(g, w, copy):
+            empty((g, w), cbn[0][g][:, w * 256:(w + 1) * 256, :], copy)
+
+        def quantize(codes, scales, src):
+            nc.vector.quantize_mx(out=codes.bitcast(FP8X4), scales=scales, in_=src.rearrange("p w t -> p (w t)"))
+
+        def q_ca(g, h):
+            cols = slice(h * H, (h + 1) * H)
+            quantize(ca_codes[:, g, cols], ca_scales[:, g, cols], nat[g][:, cols, :])
+
+        def q_cb(c, g):
+            quantize(cb_codes[:, c, g, :], cb_scales[:, c, g, :], cbn[c][g][:])
+
+        S = nc.scalar.copy
+        V = nc.vector.tensor_copy
+        widen(0, 0); turn_ca(0, 0); widen(0, 1); widen(1, 0); turn_ca(1, 0)
+        empty_ca(0, 0, 0, S); empty_ca(0, 0, 1, S)
+        widen(1, 1)
+        turn_cb(0)
+        empty_ca(1, 0, 0, S); empty_ca(1, 0, 1, S); q_ca(0, 0); empty_cb(0, 0, V); empty_cb(0, 1, S)
+        turn_cb(1); q_ca(1, 0); q_cb(0, 0)
+        empty_cb(1, 0, V); empty_cb(1, 1, S)
+        turn_ca(0, 1); turn_ca(1, 1)
+        empty_ca(0, 1, 0, S); empty_ca(0, 1, 1, S)
+        q_cb(0, 1)
+        empty_ca(1, 1, 0, V); empty_ca(1, 1, 1, S); q_ca(0, 1); q_ca(1, 1)
+
+        def energy(c):
+            for g in range(G):
+                nc.vector.tensor_tensor(out=cen[c][g][:], in0=cbn[c][g][:],
+                                        in1=ep[:, g, :].unsqueeze(1).to_broadcast([P, NC, T]), op=MULT)
+            for g in range(G):
+                quantize(cb_codes[:, 3 + c, g, :], cb_scales[:, 3 + c, g, :], cen[c][g][:])
+
+        def plain(c):
+            for g in range(G):
+                nc.vector.tensor_copy(out=cbn[c][g][:], in_=raw1[g][:, :, (c - 1) * NC:c * NC].rearrange("p t w -> p w t"))
+            for g in range(G):
+                q_cb(c, g)
+
+        energy(0); plain(1); plain(2); energy(1); energy(2)
+
+        def product(m, c, dst, on_vector):
+            acc = psum.tile([P, NC], F32, name="bank")
+            rows = slice(m * P, (m + 1) * P)
+            for g in range(G):
+                nc.tensor.matmul_mx(
+                    out=acc[:],
+                    lhsT=ca_codes[:, g, rows].bitcast(FP8X4), lhsT_scale=ca_scales[:, g, rows],
+                    rhs=cb_codes[:, c, g, :].bitcast(FP8X4), rhs_scale=cb_scales[:, c, g, :],
+                    start=(g == 0), stop=(g == G - 1))
+            if on_vector:
+                nc.vector.tensor_scalar(out=dst, in0=acc[:], scalar1=2.0, scalar2=None, op0=MULT)
+            else:
+                nc.scalar.activation(out=dst, in_=acc[:], func=COPY, scale=2.0)
+
+        for k, dram in ((0, out_p), (3, out_w)):
+            for m in range(MT):
+                o = outs.tile([P, NC], F32, name="o1")
+                product(m, k, o[:], False)
+                nc.sync.dma_start(out=dram[m * P:(m + 1) * P, 0:NC], in_=o[:])
+        for k, dram in ((0, out_p), (3, out_w)):
+            for m0 in (0, 4):
+                pair = [outs.tile([P, 2, NC], F32, name="o2") for m in range(4)]
+                for i in range(2):
+                    for m in range(4):
+                        product(m0 + m, k + 1 + i, pair[m][:, i, :], k == 3 and m % 2 == 1)
+                for m in range(4):
+                    nc.sync.dma_start(out=dram[(m0 + m) * P:(m0 + m + 1) * P, NC:3 * NC], in_=pair[m][:].rearrange("p c n -> p (c n)"))

@@ -1,7 +1,6 @@
 from contextlib import ExitStack
 
 import concourse.mybir as mybir
-from concourse.masks import make_identity
 
 F32 = mybir.dt.float32
 BF16 = mybir.dt.bfloat16
@@ -47,9 +46,6 @@ def tile_density_and_energy_weighted_block_d3_kernel(tc, ca_bytes, ca_scale, cb,
         for g in range(G):
             nc.sync.dma_start(out=raw1[g][:], in_=cbv[g, :, :, NC:3 * NC])
 
-        ident = keep.tile([P, P], BF16, name="ident")
-        make_identity(nc, ident[:])
-
         ca_codes = keep.tile([P, G, NA], U32, name="ca_codes", align_bytes=64)
         ca_scales = keep.tile([P, G, NA], U8, name="ca_scales", align_bytes=64)
         cb_codes = keep.tile([P, 6, G, NC], U32, name="cb_codes", align_bytes=64)
@@ -60,43 +56,29 @@ def tile_density_and_energy_weighted_block_d3_kernel(tc, ca_bytes, ca_scale, cb,
         cen = [[stage.tile([P, NC, T], BF16, name="cen%d" % g, align_bytes=64, bufs=2) for g in range(G)] for c in range(3)]
 
         H = NA // 2
-        banks = {}
 
-        def widen(g, h):
+        def widen(g, h, planes, on_vector):
             cols = slice(h * H, (h + 1) * H)
-            for t in (3, 0, 1, 2):
+            for t in planes:
                 src = byt[g][:, t, cols].bitcast(FP8)
-                if t == 3:
-                    nc.scalar.activation(out=wide[g][:, t, cols], in_=src, func=COPY, scale=sc[:, g, t:t + 1])
-                else:
+                if on_vector:
                     nc.vector.tensor_scalar(out=wide[g][:, t, cols], in0=src, scalar1=sc[:, g, t:t + 1], scalar2=None, op0=MULT)
+                else:
+                    nc.scalar.activation(out=wide[g][:, t, cols], in_=src, func=COPY, scale=sc[:, g, t:t + 1])
 
-        def turn(key, src, w0):
-            bank = psum.tile([P, 2, P, T], BF16, name="bank")
-            for i in range(2):
-                nc.tensor.matmul(
-                    out=bank[:, i], lhsT=ident[:],
-                    rhs=src[:, :, w0 + i * P:w0 + (i + 1) * P].rearrange("p t w -> p w t"),
-                    start=True, stop=True)
-            banks[key] = bank
+        S = nc.scalar.copy
+        V = nc.vector.tensor_copy
 
-        def empty(key, dst, copy):
-            copy(out=dst, in_=banks[key][:].rearrange("p i w t -> p (i w) t"))
+        def turn(dst, src, copy):
+            copy(out=dst, in_=src.rearrange("p t w -> p w t"))
 
-        def turn_ca(g, h):
-            for w in range(2):
-                turn((g, h, w), wide[g], h * H + w * 256)
+        def turn_ca(g, h, copy):
+            cols = slice(h * H, (h + 1) * H)
+            turn(nat[g][:, cols, :], wide[g][:, :, cols], copy)
 
-        def empty_ca(g, h, w, copy):
-            w0 = h * H + w * 256
-            empty((g, h, w), nat[g][:, w0:w0 + 256, :], copy)
-
-        def turn_cb(g):
-            for w in range(2):
-                turn((g, w), raw0[g], w * 256)
-
-        def empty_cb(g, w, copy):
-            empty((g, w), cbn[0][g][:, w * 256:(w + 1) * 256, :], copy)
+        def turn_cb(c, g, copy):
+            src = raw0[g][:] if c == 0 else raw1[g][:, :, (c - 1) * NC:c * NC]
+            turn(cbn[c][g][:], src, copy)
 
         def quantize(codes, scales, src):
             nc.vector.quantize_mx(out=codes.bitcast(FP8X4), scales=scales, in_=src.rearrange("p w t -> p (w t)"))
@@ -108,20 +90,6 @@ def tile_density_and_energy_weighted_block_d3_kernel(tc, ca_bytes, ca_scale, cb,
         def q_cb(c, g):
             quantize(cb_codes[:, c, g, :], cb_scales[:, c, g, :], cbn[c][g][:])
 
-        S = nc.scalar.copy
-        V = nc.vector.tensor_copy
-        widen(0, 0); turn_ca(0, 0); widen(0, 1); widen(1, 0); turn_ca(1, 0)
-        empty_ca(0, 0, 0, S); empty_ca(0, 0, 1, S)
-        widen(1, 1)
-        turn_cb(0)
-        empty_ca(1, 0, 0, S); empty_ca(1, 0, 1, S); q_ca(0, 0); empty_cb(0, 0, V); empty_cb(0, 1, S)
-        turn_cb(1); q_ca(1, 0); q_cb(0, 0)
-        empty_cb(1, 0, V); empty_cb(1, 1, S)
-        turn_ca(0, 1); turn_ca(1, 1)
-        empty_ca(0, 1, 0, S); empty_ca(0, 1, 1, S)
-        q_cb(0, 1)
-        empty_ca(1, 1, 0, V); empty_ca(1, 1, 1, S); q_ca(0, 1); q_ca(1, 1)
-
         def energy(c):
             for g in range(G):
                 nc.vector.tensor_tensor(out=cen[c][g][:], in0=cbn[c][g][:],
@@ -131,11 +99,9 @@ def tile_density_and_energy_weighted_block_d3_kernel(tc, ca_bytes, ca_scale, cb,
 
         def plain(c):
             for g in range(G):
-                nc.vector.tensor_copy(out=cbn[c][g][:], in_=raw1[g][:, :, (c - 1) * NC:c * NC].rearrange("p t w -> p w t"))
+                turn_cb(c, g, V)
             for g in range(G):
                 q_cb(c, g)
-
-        energy(0); plain(1); plain(2); energy(1); energy(2)
 
         def product(m, c, dst, on_vector):
             acc = psum.tile([P, NC], F32, name="bank")
@@ -151,11 +117,29 @@ def tile_density_and_energy_weighted_block_d3_kernel(tc, ca_bytes, ca_scale, cb,
             else:
                 nc.scalar.activation(out=dst, in_=acc[:], func=COPY, scale=2.0)
 
-        for k, dram in ((0, out_p), (3, out_w)):
-            for m in range(MT):
+        def single(k, ms):
+            dram, c = ((out_p, k) if k < 3 else (out_w, k - 3))
+            for m in ms:
                 o = outs.tile([P, NC], F32, name="o1")
                 product(m, k, o[:], False)
-                nc.sync.dma_start(out=dram[m * P:(m + 1) * P, 0:NC], in_=o[:])
+                nc.sync.dma_start(out=dram[m * P:(m + 1) * P, c * NC:(c + 1) * NC], in_=o[:])
+
+        for g in range(G):
+            widen(g, 0, (3, 2), False); widen(g, 0, (0, 1), True)
+        turn_ca(0, 0, V); turn_ca(1, 0, S)
+        turn_cb(0, 0, V); turn_cb(0, 1, V)
+        q_ca(0, 0); q_cb(0, 0); q_ca(1, 0); q_cb(0, 1)
+        for g in range(G):
+            widen(g, 1, (3, 2), False)
+        for g in range(G):
+            widen(g, 1, (0, 1), True)
+        single(0, range(0, 4))
+        energy(0)
+        turn_ca(1, 1, S); turn_ca(0, 1, V)
+        single(3, range(0, 4))
+        q_ca(0, 1); q_ca(1, 1)
+        single(0, range(4, 8)); single(3, range(4, 8))
+        plain(1); plain(2); energy(1); energy(2)
         for k, dram in ((0, out_p), (3, out_w)):
             for m0 in (0, 4):
                 pair = [outs.tile([P, 2, NC], F32, name="o2") for m in range(4)]

@@ -34,13 +34,14 @@ def tile_density_and_energy_weighted_block_d3_kernel(tc, ca_bytes, ca_scale, cb,
         ep = keep.tile([P, G, T], BF16, name="ep")
         nc.scalar.dma_start(out=sc[:], in_=ca_scale.rearrange("(g p t) o -> p g (t o)", p=P, t=T))
         nc.scalar.dma_start(out=ep[:], in_=eps.rearrange("(g p t) -> p g t", p=P, t=T))
-        cav = ca_bytes.rearrange("(g p t) n -> g p t n", p=P, t=T)
+        cav = ca_bytes.rearrange("(g p u t) n -> g u p t n", p=P, u=2, t=2)
         cbv = cb.rearrange("(g p t) n -> g p t n", p=P, t=T)
-        byt = [keep.tile([P, T, NA], U8, name="byt%d" % g) for g in range(G)]
+        byt = [[keep.tile([P, 2, NA], U8, name="byt%d_%d" % (g, u)) for u in range(2)] for g in range(G)]
         raw0 = [keep.tile([P, T, NC], BF16, name="rawa%d" % g) for g in range(G)]
         raw1 = [keep.tile([P, T, 2 * NC], BF16, name="rawb%d" % g) for g in range(G)]
         for g in range(G):
-            nc.sync.dma_start(out=byt[g][:], in_=cav[g])
+            for u in range(2):
+                nc.sync.dma_start(out=byt[g][u][:], in_=cav[g, u])
         for g in range(G):
             nc.sync.dma_start(out=raw0[g][:], in_=cbv[g, :, :, 0:NC])
         for g in range(G):
@@ -60,7 +61,7 @@ def tile_density_and_energy_weighted_block_d3_kernel(tc, ca_bytes, ca_scale, cb,
         def widen(g, h, planes, on_vector):
             cols = slice(h * H, (h + 1) * H)
             for t in planes:
-                src = byt[g][:, t, cols].bitcast(FP8)
+                src = byt[g][t // 2][:, t % 2, cols].bitcast(FP8)
                 if on_vector:
                     nc.vector.tensor_scalar(out=wide[g][:, t, cols], in0=src, scalar1=sc[:, g, t:t + 1], scalar2=None, op0=MULT)
                 else:
@@ -70,7 +71,7 @@ def tile_density_and_energy_weighted_block_d3_kernel(tc, ca_bytes, ca_scale, cb,
         V = nc.vector.tensor_copy
 
         def turn(dst, src, copy):
-            copy(out=dst, in_=src.rearrange("p t w -> p w t"))
+            copy(out=dst.rearrange("p (c i) t -> p c t i", i=4), in_=src.rearrange("p t (c i) -> p c t i", i=4))
 
         def turn_ca(g, h, copy):
             cols = slice(h * H, (h + 1) * H)
@@ -124,15 +125,16 @@ def tile_density_and_energy_weighted_block_d3_kernel(tc, ca_bytes, ca_scale, cb,
                 product(m, k, o[:], False)
                 nc.sync.dma_start(out=dram[m * P:(m + 1) * P, c * NC:(c + 1) * NC], in_=o[:])
 
-        for g in range(G):
-            widen(g, 0, (3, 2), False); widen(g, 0, (0, 1), True)
+        widen(0, 0, (0, 2), False)
+        for t in (1, 3):
+            widen(0, 0, (t,), True); widen(0, 1, (t,), True)
+        widen(1, 0, (0, 2), False); widen(1, 0, (1, 3), True)
         turn_ca(0, 0, V); turn_ca(1, 0, S)
-        turn_cb(0, 0, V); turn_cb(0, 1, V)
+        turn_cb(0, 0, V)
+        widen(0, 1, (0, 2), False)
+        turn_cb(0, 1, V)
         q_ca(0, 0); q_cb(0, 0); q_ca(1, 0); q_cb(0, 1)
-        for g in range(G):
-            widen(g, 1, (3, 2), False)
-        for g in range(G):
-            widen(g, 1, (0, 1), True)
+        widen(1, 1, (0, 2, 1), False); widen(1, 1, (3,), True)
         single(0, range(0, 4))
         energy(0)
         turn_ca(1, 1, S); turn_ca(0, 1, V)
@@ -140,11 +142,18 @@ def tile_density_and_energy_weighted_block_d3_kernel(tc, ca_bytes, ca_scale, cb,
         q_ca(0, 1); q_ca(1, 1)
         single(0, range(4, 8)); single(3, range(4, 8))
         plain(1); plain(2); energy(1); energy(2)
-        for k, dram in ((0, out_p), (3, out_w)):
-            for m0 in (0, 4):
-                pair = [outs.tile([P, 2, NC], F32, name="o2") for m in range(4)]
-                for i in range(2):
-                    for m in range(4):
-                        product(m0 + m, k + 1 + i, pair[m][:, i, :], k == 3 and m % 2 == 1)
-                for m in range(4):
-                    nc.sync.dma_start(out=dram[(m0 + m) * P:(m0 + m + 1) * P, NC:3 * NC], in_=pair[m][:].rearrange("p c n -> p (c n)"))
+
+        def store_pair(dram, m, pair):
+            nc.sync.dma_start(out=dram[m * P:(m + 1) * P, NC:3 * NC], in_=pair[:].rearrange("p c n -> p (c n)"))
+
+        single(1, range(MT)); single(2, range(MT))
+        for m in range(MT):
+            pair = outs.tile([P, 2, NC], F32, name="o2")
+            product(m, 4, pair[:, 0, :], False)
+            if m == MT - 1:
+                nc.sync.dma_start(out=out_w[m * P:, NC:2 * NC], in_=pair[:, 0, :])
+            product(m, 5, pair[:, 1, :], True)
+            if m == MT - 1:
+                nc.sync.dma_start(out=out_w[m * P:, 2 * NC:], in_=pair[:, 1, :])
+            else:
+                store_pair(out_w, m, pair)

@@ -51,8 +51,8 @@ def tile_density_and_energy_weighted_block_d3_kernel(tc, ca_bytes, ca_scale, cb,
         ca_scales = keep.tile([P, G, NA], U8, name="ca_scales", align_bytes=64)
         cb_codes = keep.tile([P, 6, G, NC], U32, name="cb_codes", align_bytes=64)
         cb_scales = keep.tile([P, 6, G, NC], U8, name="cb_scales", align_bytes=64)
-        wide = [keep.tile([P, T, NA], BF16, name="wide%d" % g) for g in range(G)]
-        nat = [keep.tile([P, NA, T], BF16, name="nat%d" % g, align_bytes=64) for g in range(G)]
+        wide = [[keep.tile([P, T, NA // 2], BF16, name="wide%d_%d" % (g, h)) for h in range(2)] for g in range(G)]
+        nat = [[keep.tile([P, NA // 2, T], BF16, name="nat%d_%d" % (g, h), align_bytes=64) for h in range(2)] for g in range(G)]
         cbn = [[keep.tile([P, NC, T], BF16, name="cbn%d_%d" % (c, g), align_bytes=64) for g in range(G)] for c in range(3)]
         cen = [[stage.tile([P, NC, T], BF16, name="cen%d" % g, align_bytes=64, bufs=2) for g in range(G)] for c in range(3)]
 
@@ -63,9 +63,9 @@ def tile_density_and_energy_weighted_block_d3_kernel(tc, ca_bytes, ca_scale, cb,
             for t in planes:
                 src = byt[g][t // 2][:, t % 2, cols].bitcast(FP8)
                 if on_vector:
-                    nc.vector.tensor_scalar(out=wide[g][:, t, cols], in0=src, scalar1=sc[:, g, t:t + 1], scalar2=None, op0=MULT)
+                    nc.vector.tensor_scalar(out=wide[g][h][:, t, :], in0=src, scalar1=sc[:, g, t:t + 1], scalar2=None, op0=MULT)
                 else:
-                    nc.scalar.activation(out=wide[g][:, t, cols], in_=src, func=COPY, scale=sc[:, g, t:t + 1])
+                    nc.scalar.activation(out=wide[g][h][:, t, :], in_=src, func=COPY, scale=sc[:, g, t:t + 1])
 
         S = nc.scalar.copy
         V = nc.vector.tensor_copy
@@ -74,8 +74,7 @@ def tile_density_and_energy_weighted_block_d3_kernel(tc, ca_bytes, ca_scale, cb,
             copy(out=dst.rearrange("p (c i) t -> p c t i", i=4), in_=src.rearrange("p t (c i) -> p c t i", i=4))
 
         def turn_ca(g, h, copy):
-            cols = slice(h * H, (h + 1) * H)
-            turn(nat[g][:, cols, :], wide[g][:, :, cols], copy)
+            turn(nat[g][h][:], wide[g][h][:], copy)
 
         def turn_cb(c, g, copy):
             src = raw0[g][:] if c == 0 else raw1[g][:, :, (c - 1) * NC:c * NC]
@@ -86,7 +85,7 @@ def tile_density_and_energy_weighted_block_d3_kernel(tc, ca_bytes, ca_scale, cb,
 
         def q_ca(g, h):
             cols = slice(h * H, (h + 1) * H)
-            quantize(ca_codes[:, g, cols], ca_scales[:, g, cols], nat[g][:, cols, :])
+            quantize(ca_codes[:, g, cols], ca_scales[:, g, cols], nat[g][h][:])
 
         def q_cb(c, g):
             quantize(cb_codes[:, c, g, :], cb_scales[:, c, g, :], cbn[c][g][:])
@@ -126,18 +125,20 @@ def tile_density_and_energy_weighted_block_d3_kernel(tc, ca_bytes, ca_scale, cb,
                 nc.sync.dma_start(out=dram[m * P:(m + 1) * P, c * NC:(c + 1) * NC], in_=o[:])
 
         widen(0, 0, (0, 2), False)
-        for t in (1, 3):
-            widen(0, 0, (t,), True); widen(0, 1, (t,), True)
-        widen(1, 0, (0, 2), False); widen(1, 0, (1, 3), True)
+        widen(0, 0, (1, 3), True)
+        widen(0, 1, (1, 3, 2), True)
+        widen(1, 0, (0, 2), False)
+        widen(1, 0, (1, 3), True)
         turn_ca(0, 0, V); turn_ca(1, 0, S)
         turn_cb(0, 0, V)
-        widen(0, 1, (0, 2), False)
+        widen(1, 1, (0, 2, 3, 1), False)
         turn_cb(0, 1, V)
+        widen(0, 1, (0,), False)
+        turn_ca(1, 1, S)
         q_ca(0, 0); q_cb(0, 0); q_ca(1, 0); q_cb(0, 1)
-        widen(1, 1, (0, 2, 1), False); widen(1, 1, (3,), True)
         single(0, range(0, 4))
         energy(0)
-        turn_ca(1, 1, S); turn_ca(0, 1, V)
+        turn_ca(0, 1, V)
         single(3, range(0, 4))
         q_ca(0, 1); q_ca(1, 1)
         single(0, range(4, 8)); single(3, range(4, 8))
@@ -147,13 +148,13 @@ def tile_density_and_energy_weighted_block_d3_kernel(tc, ca_bytes, ca_scale, cb,
             nc.sync.dma_start(out=dram[m * P:(m + 1) * P, NC:3 * NC], in_=pair[:].rearrange("p c n -> p (c n)"))
 
         single(1, range(MT)); single(2, range(MT))
-        for m in range(MT):
+        for m in range(MT - 2):
             pair = outs.tile([P, 2, NC], F32, name="o2")
             product(m, 4, pair[:, 0, :], False)
-            if m == MT - 1:
-                nc.sync.dma_start(out=out_w[m * P:, NC:2 * NC], in_=pair[:, 0, :])
             product(m, 5, pair[:, 1, :], True)
-            if m == MT - 1:
-                nc.sync.dma_start(out=out_w[m * P:, 2 * NC:], in_=pair[:, 1, :])
-            else:
-                store_pair(out_w, m, pair)
+            store_pair(out_w, m, pair)
+        for m in range(MT - 2, MT):
+            for k in (4, 5):
+                o = outs.tile([P, NC], F32, name="o1")
+                product(m, k, o[:], k == 5)
+                nc.sync.dma_start(out=out_w[m * P:(m + 1) * P, (k - 3) * NC:(k - 2) * NC], in_=o[:])

@@ -92,8 +92,10 @@ def tile_density_and_energy_weighted_block_d3_kernel(tc, ca_bytes, ca_scale, cb,
 
         def energy(c):
             for g in range(G):
-                nc.vector.tensor_tensor(out=cen[c][g][:], in0=cbn[c][g][:],
-                                        in1=ep[:, g, :].unsqueeze(1).to_broadcast([P, NC, T]), op=MULT)
+                nc.vector.tensor_tensor(
+                    out=cen[c][g][:].rearrange("p (r w) t -> p r (w t)", w=P),
+                    in0=cbn[c][g][:].rearrange("p (r w) t -> p r (w t)", w=P),
+                    in1=epr[:, g].rearrange("p w t -> p (w t)").unsqueeze(1).to_broadcast([P, NC // P, P * T]), op=MULT)
             for g in range(G):
                 quantize(cb_codes[:, 3 + c, g, :], cb_scales[:, 3 + c, g, :], cen[c][g][:])
 
@@ -129,6 +131,8 @@ def tile_density_and_energy_weighted_block_d3_kernel(tc, ca_bytes, ca_scale, cb,
         widen(0, 1, (1, 3, 2), True)
         widen(1, 0, (0, 2), False)
         widen(1, 0, (1, 3), True)
+        epr = keep.tile([P, G, P, T], BF16, name="epr")
+        nc.vector.tensor_copy(out=epr[:], in_=ep[:].unsqueeze(2).to_broadcast([P, G, P, T]))
         turn_ca(0, 0, V); turn_ca(1, 0, S)
         turn_cb(0, 0, V)
         widen(1, 1, (0, 2, 3, 1), False)

from contextlib import ExitStack

import concourse.mybir as mybir

F32 = mybir.dt.float32
BF16 = mybir.dt.bfloat16
U32 = mybir.dt.uint32
U8 = mybir.dt.uint8
FP8 = mybir.dt.float8_e4m3fn
FP8X4 = mybir.dt.float8_e4m3fn_x4
COPY = mybir.ActivationFunctionType.Copy
MULT = mybir.AluOpType.mult

O, NA, NB = 1024, 1024, 1536
FLOPS = 2 * 2 * O * NA * NB

P = 128
T = 4
G = O // (P * T)
NC = 512
MT = NA // P


def tile_density_and_energy_weighted_block_d3_kernel(tc, ca_bytes, ca_scale, cb, eps, out_p, out_w):
    nc = tc.nc
    with ExitStack() as ctx:
        keep = ctx.enter_context(tc.tile_pool(name="keep", bufs=1))
        stage = ctx.enter_context(tc.tile_pool(name="stage", bufs=1))
        outs = ctx.enter_context(tc.tile_pool(name="outs", bufs=8))
        psum = ctx.enter_context(tc.psum_pool(name="psum", bufs=8))
        ctx.enter_context(tc.manual_schedule())

        sc = keep.tile([P, G, T], F32, name="sc")
        ep = keep.tile([P, G, T], BF16, name="ep")
        nc.scalar.dma_start(out=sc[:], in_=ca_scale.rearrange("(g p t) o -> p g (t o)", p=P, t=T))
        nc.scalar.dma_start(out=ep[:], in_=eps.rearrange("(g p t) -> p g t", p=P, t=T))
        cav = ca_bytes.rearrange("(g p u t) n -> g u p t n", p=P, u=2, t=2)
        cbv = cb.rearrange("(g p t) n -> g p t n", p=P, t=T)
        byt = [[keep.tile([P, 2, NA], U8, name="byt%d_%d" % (g, u)) for u in range(2)] for g in range(G)]
        raw0 = [keep.tile([P, T, NC], BF16, name="rawa%d" % g) for g in range(G)]
        raw1 = [keep.tile([P, T, 2 * NC], BF16, name="rawb%d" % g) for g in range(G)]
        for g in range(G):
            for u in range(2):
                nc.sync.dma_start(out=byt[g][u][:], in_=cav[g, u])
        for g in range(G):
            nc.sync.dma_start(out=raw0[g][:], in_=cbv[g, :, :, 0:NC])
        for g in range(G):
            nc.sync.dma_start(out=raw1[g][:], in_=cbv[g, :, :, NC:3 * NC])

        ca_codes = keep.tile([P, G, NA], U32, name="ca_codes", align_bytes=64)
        ca_scales = keep.tile([P, G, NA], U8, name="ca_scales", align_bytes=64)
        cb_codes = keep.tile([P, 6, G, NC], U32, name="cb_codes", align_bytes=64)
        cb_scales = keep.tile([P, 6, G, NC], U8, name="cb_scales", align_bytes=64)
        wide = [[keep.tile([P, T, NA // 2], BF16, name="wide%d_%d" % (g, h)) for h in range(2)] for g in range(G)]
        nat = [[keep.tile([P, NA // 2, T], BF16, name="nat%d_%d" % (g, h), align_bytes=64) for h in range(2)] for g in range(G)]
        cbn = [[keep.tile([P, NC, T], BF16, name="cbn%d_%d" % (c, g), align_bytes=64) for g in range(G)] for c in range(3)]
        cen = [[stage.tile([P, NC, T], BF16, name="cen%d" % g, align_bytes=64, bufs=2) for g in range(G)] for c in range(3)]

        H = NA // 2

        def widen(g, h, planes, on_vector):
            cols = slice(h * H, (h + 1) * H)
            for t in planes:
                src = byt[g][t // 2][:, t % 2, cols].bitcast(FP8)
                if on_vector:
                    nc.vector.tensor_scalar(out=wide[g][h][:, t, :], in0=src, scalar1=sc[:, g, t:t + 1], scalar2=None, op0=MULT)
                else:
                    nc.scalar.activation(out=wide[g][h][:, t, :], in_=src, func=COPY, scale=sc[:, g, t:t + 1])

        S = nc.scalar.copy
        V = nc.vector.tensor_copy

        def turn(dst, src, copy):
            copy(out=dst.rearrange("p (c i) t -> p c t i", i=4), in_=src.rearrange("p t (c i) -> p c t i", i=4))

        def turn_ca(g, h, copy):
            turn(nat[g][h][:], wide[g][h][:], copy)

        def turn_cb(c, g, copy):
            src = raw0[g][:] if c == 0 else raw1[g][:, :, (c - 1) * NC:c * NC]
            turn(cbn[c][g][:], src, copy)

        def quantize(codes, scales, src):
            nc.vector.quantize_mx(out=codes.bitcast(FP8X4), scales=scales, in_=src.rearrange("p w t -> p (w t)"))

        def q_ca(g, h):
            cols = slice(h * H, (h + 1) * H)
            quantize(ca_codes[:, g, cols], ca_scales[:, g, cols], nat[g][h][:])

        def q_cb(c, g):
            quantize(cb_codes[:, c, g, :], cb_scales[:, c, g, :], cbn[c][g][:])

        def energy(c):
            for g in range(G):
                nc.vector.tensor_tensor(
                    out=cen[c][g][:].rearrange("p (r w) t -> p r (w t)", w=P),
                    in0=cbn[c][g][:].rearrange("p (r w) t -> p r (w t)", w=P),
                    in1=epr[:, g].rearrange("p w t -> p (w t)").unsqueeze(1).to_broadcast([P, NC // P, P * T]), op=MULT)
            for g in range(G):
                quantize(cb_codes[:, 3 + c, g, :], cb_scales[:, 3 + c, g, :], cen[c][g][:])

        def plain(c):
            for g in range(G):
                turn_cb(c, g, V)
            for g in range(G):
                q_cb(c, g)

        def product(m, c, dst, on_vector):
            acc = psum.tile([P, NC], F32, name="bank")
            rows = slice(m * P, (m + 1) * P)
            for g in range(G):
                nc.tensor.matmul_mx(
                    out=acc[:],
                    lhsT=ca_codes[:, g, rows].bitcast(FP8X4), lhsT_scale=ca_scales[:, g, rows],
                    rhs=cb_codes[:, c, g, :].bitcast(FP8X4), rhs_scale=cb_scales[:, c, g, :],
                    start=(g == 0), stop=(g == G - 1))
            if on_vector:
                nc.vector.tensor_scalar(out=dst, in0=acc[:], scalar1=2.0, scalar2=None, op0=MULT)
            else:
                nc.scalar.activation(out=dst, in_=acc[:], func=COPY, scale=2.0)

        def single(k, ms):
            dram, c = ((out_p, k) if k < 3 else (out_w, k - 3))
            for m in ms:
                o = outs.tile([P, NC], F32, name="o1")
                product(m, k, o[:], False)
                nc.sync.dma_start(out=dram[m * P:(m + 1) * P, c * NC:(c + 1) * NC], in_=o[:])

        widen(0, 0, (0, 2), False)
        widen(0, 0, (1, 3), True)
        widen(0, 1, (1, 3, 2), True)
        widen(1, 0, (0, 2), False)
        widen(1, 0, (1, 3), True)
        epr = keep.tile([P, G, P, T], BF16, name="epr")
        nc.vector.tensor_copy(out=epr[:], in_=ep[:].unsqueeze(2).to_broadcast([P, G, P, T]))
        turn_ca(0, 0, V); turn_ca(1, 0, S)
        turn_cb(0, 0, V)
        widen(1, 1, (0, 2, 3, 1), False)
        turn_cb(0, 1, V)
        widen(0, 1, (0,), False)
        turn_ca(1, 1, S)
        q_ca(0, 0); q_cb(0, 0); q_ca(1, 0); q_cb(0, 1)
        single(0, range(0, 4))
        energy(0)
        turn_ca(0, 1, V)
        single(3, range(0, 4))
        q_ca(0, 1); q_ca(1, 1)
        single(0, range(4, 8)); single(3, range(4, 8))
        plain(1); plain(2); energy(1); energy(2)

        def store_pair(dram, m, pair):
            nc.sync.dma_start(out=dram[m * P:(m + 1) * P, NC:3 * NC], in_=pair[:].rearrange("p c n -> p (c n)"))

        single(1, range(MT)); single(2, range(MT))
        for m in range(MT - 2):
            pair = outs.tile([P, 2, NC], F32, name="o2")
            product(m, 4, pair[:, 0, :], False)
            product(m, 5, pair[:, 1, :], True)
            store_pair(out_w, m, pair)
        for m in range(MT - 2, MT):
            for k in (4, 5):
                o = outs.tile([P, NC], F32, name="o1")
                product(m, k, o[:], k == 5)
                nc.sync.dma_start(out=out_w[m * P:(m + 1) * P, (k - 3) * NC:(k - 2) * NC], in_=o[:])
